import numpy as np
import ml_dtypes


def mxq(x, axis, fmt="e4m3"):
    dtype, down = {"e4m3": (ml_dtypes.float8_e4m3fn, 7), "e5m2": (ml_dtypes.float8_e5m2, 14)}[fmt]
    v = np.moveaxis(np.asarray(x, np.float32).astype(ml_dtypes.bfloat16).astype(np.float64), axis, -1)
    blocks = v.reshape(v.shape[:-1] + (-1, 32))
    amax = np.abs(blocks).max(-1, keepdims=True)
    byte = np.maximum(np.where(amax > 0, np.frexp(amax)[1] - 1 + 127, 0) - down, 1)
    scale = np.exp2(byte - 127.0)
    codes = (blocks / scale).astype(np.float32).astype(dtype).astype(np.float64)
    return np.moveaxis((codes * scale).reshape(v.shape), -1, axis)


WIDE = False


def mx_kscale(k):
    if not WIDE:
        return np.ones(k)
    levels = np.array([10, -10, 5, -5, 0])
    if k % 512:
        return np.exp2(np.random.permutation(np.resize(levels, k // 32))).repeat(32)
    a = np.empty((k // 512, 16))
    for p in range(k // 512):
        a[p, :8] = np.random.permutation(np.resize(levels, 8))
        for g in range(8):
            far = levels[np.abs(levels - a[p, g]) >= 10]
            a[p, g + 8] = far[np.random.randint(len(far))]
    return np.exp2(a.ravel()).repeat(32)


def f64(x):
    return np.asarray(x).astype(np.float64)


def striped(idx):
    return np.tile(idx.reshape(-1, 16).T, (8, 1)).astype(np.uint16)


def unstriped(offs):
    return offs[:16].T.reshape(-1).astype(np.int64)


def pack_weight(w):
    k, n = w.shape
    w = f64(np.asarray(w, np.float32).astype(ml_dtypes.bfloat16)).reshape(k // 32, 32, n)
    amax = np.abs(w).max(1)
    byte = np.clip(np.where(amax > 0, np.frexp(amax)[1] - 1 + 127 - 7, 1), 1, 254)
    scaled = (w * np.exp2(127.0 - byte)[:, None, :]).reshape(k, n).astype(np.float32)
    words = np.ascontiguousarray(scaled.reshape(k // 512, 128, 4, n).transpose(0, 1, 3, 2)).astype(ml_dtypes.float8_e4m3fn).view(np.uint8)
    return words, np.ascontiguousarray(byte.astype(np.uint8).reshape(k // 512, 16, n))


def unpack_weight(words, scales):
    g, p, n, _ = words.shape
    vals = np.ascontiguousarray(words).view(ml_dtypes.float8_e4m3fn).astype(np.float64) * np.repeat(np.exp2(scales.astype(np.float64) - 127.0), 8, axis=1)[..., None]
    return vals.transpose(0, 1, 3, 2).reshape(g * 512, n)


def relu(v):
    return np.maximum(v, 0.0)


K, T, S, D, N, H, V, U = 1024, 2048, 1024, 4, 128, 512, 256, 512


def setup_inputs():
    n = np.random.standard_normal
    s = mx_kscale(K)[:, None]
    u = mx_kscale(H)
    packed_xT = pack_weight(n((K, T)) * s)
    return {
        "x_words": packed_xT[0],
        "x_scales": packed_xT[1],
        "w1": (n((K, H)) / np.sqrt(K) / s).astype(np.float32),
        "w2": (n((K, H)) / np.sqrt(K) / s).astype(np.float32),
        "dz": (np.random.uniform(0.3, 1.2, (H, S))).astype(np.float32),
        "unit": (np.random.uniform(0.6, 1.4, (H, 1)) * u[:, None]).astype(np.float32),
        "w3": (n((H, N)) / np.sqrt(H) / u[:, None]).astype(np.float32),
        "offs": striped(np.random.permutation(T)[:S]),
        "env": striped(np.random.permutation(S)),
        "stn": striped(np.random.permutation(np.concatenate([np.arange(V), np.random.randint(0, V, U - V)]))),
    }


def reference(x_words, x_scales, w1, w2, dz, unit, w3, offs, env, stn):
    xq = unpack_weight(x_words, x_scales)[:, unstriped(offs)]
    tp = mxq(f64(w1), 0, "e4m3").T @ xq
    temp = np.tanh(tp)
    wv = mxq(f64(w2), 0, "e4m3").T @ xq
    moist = np.log(np.exp(wv) + 1.0)
    thetae = (temp + 1.5) * (np.exp(0.6 * np.tanh(moist)))
    te = thetae[:, unstriped(env)]
    buoy = thetae - te
    cl_ = relu(buoy) * f64(dz)
    cape = cl_.reshape(len(cl_), -1, D).sum(axis=2)
    cs = cape[:, unstriped(stn)]
    nb_ = relu(-1.0 * buoy)
    cin = nb_.reshape(len(nb_), -1, D).max(axis=2)
    is_ = cin[:, unstriped(stn)]
    hid = f64(unit) * (np.sqrt(cs + 0.1) - is_)
    return mxq(f64(w3), 0, "e4m3").T @ mxq(hid, 0, "e4m3")

@@ -1,0 +1,266 @@
+from contextlib import ExitStack
+
+import concourse.mybir as mybir
+from concourse.masks import make_identity
+
+K, T, S, D, N, H, V, U = 1024, 2048, 1024, 4, 128, 512, 256, 512
+FLOPS = 2 * (2 * K * H * S + H * N * U)
+
+F32 = mybir.dt.float32
+BF16 = mybir.dt.bfloat16
+I32 = mybir.dt.int32
+U32 = mybir.dt.uint32
+U16 = mybir.dt.uint16
+U8 = mybir.dt.uint8
+FP8X4 = mybir.dt.float8_e4m3fn_x4
+ALU = mybir.AluOpType
+ACT = mybir.ActivationFunctionType
+
+P = 128
+PACK = 4
+PASSES = K // (P * PACK)
+HALF = 512
+HALVES = S // HALF
+TINY = 2.0 ** -60
+DIRECT = 768
+ENV = "VVVAAAAA"
+STN = "AASS"
+LAG = 3
+
+
+def tile_picked_yweathr_upd_p_kernel(tc, x_words, x_scales, w1, w2, dz, unit, w3, offs, env, stn, out):
+    nc = tc.nc
+    with ExitStack() as ctx:
+        keep = ctx.enter_context(tc.tile_pool(name="keep", bufs=1))
+        ring = ctx.enter_context(tc.tile_pool(name="ring", bufs=2))
+        psum = ctx.enter_context(tc.psum_pool(name="psum", bufs=8))
+
+        offs_sb = keep.tile([P, S // 16], U16, name="offs_sb")
+        env_sb = keep.tile([P, S // 16], U16, name="env_sb")
+        stn_sb = keep.tile([P, U // 16], U16, name="stn_sb")
+        x_table = [keep.tile([P, T], I32, name=f"x_table{o}") for o in range(PASSES)]
+        scale_table = keep.tile([P, T], U8, name="scale_table")
+        w_raw = {(a, o): keep.tile([P, PACK, H], F32, name=f"w_raw{a}{o}") for a in (1, 2) for o in range(PASSES)}
+        dz_sb = [keep.tile([P, S], F32, name=f"dz{t}") for t in range(PACK)]
+        unit_sb = keep.tile([P, PACK], F32, name="unit_sb")
+        w3_raw = keep.tile([P, PACK, N], F32, name="w3_raw")
+
+        def load_w(a, w, o):
+            nc.sync.dma_start(out=w_raw[a, o][:], in_=w[512 * o : 512 * (o + 1), :].rearrange("(p j) c -> p j c", j=PACK))
+
+        def load_x(o):
+            nc.sync.dma_start(out=x_table[o][:], in_=x_words[o].rearrange("p n t -> p (n t)").bitcast(I32))
+
+        nc.vector.memset(scale_table[:].bitcast(I32), 0)
+        nc.sync.dma_start(offs_sb[:], offs)
+        load_w(2, w2, 0)
+        for q in range(4):
+            nc.sync.dma_start(out=scale_table[32 * q : 32 * q + 8, :].bitcast(I32), in_=x_scales[:, 4 * q : 4 * q + 4, :].bitcast(I32))
+        load_x(0)
+        load_w(2, w2, 1)
+        load_x(1)
+        load_w(1, w1, 0)
+        load_w(1, w1, 1)
+        nc.sync.dma_start(env_sb[:], env)
+        dz_rows = dz.rearrange("(p t) s -> p t s", t=PACK)
+        for t in range(PACK):
+            nc.sync.dma_start(out=dz_sb[t][:], in_=dz_rows[:, t, :])
+        nc.sync.dma_start(stn_sb[:], stn)
+        nc.sync.dma_start(out=unit_sb[:], in_=unit.rearrange("(p t) o -> p (t o)", t=PACK))
+        nc.sync.dma_start(out=w3_raw[:], in_=w3.rearrange("(p j) n -> p j n", j=PACK))
+
+        w_bf = {key: keep.tile([P, PACK, P, PACK], BF16, name=f"w_bf{key[0]}{key[1]}", align_bytes=64) for key in w_raw}
+        w_codes = {key: keep.tile([P, H], U32, name=f"w_codes{key[0]}{key[1]}", align_bytes=64) for key in w_raw}
+        w_scales = {key: keep.tile([P, H], U8, name=f"w_scales{key[0]}{key[1]}", align_bytes=64) for key in w_raw}
+
+        def round_w(copy, key, t0, t1):
+            copy(
+                out=w_bf[key][:, t0:t1].rearrange("p t m j -> p m t j"),
+                in_=w_raw[key][:].rearrange("p j (m t) -> p m t j", t=PACK)[:, :, t0:t1, :],
+            )
+
+        def quantize_w(key, t0, t1):
+            nc.vector.quantize_mx(
+                out=w_codes[key][:, P * t0 : P * t1].bitcast(FP8X4),
+                scales=w_scales[key][:, P * t0 : P * t1],
+                in_=w_bf[key][:, t0:t1].rearrange("p t m j -> p (t m j)"),
+            )
+
+        x_scale = keep.tile([P, S], U8, name="x_scale", align_bytes=64)
+        x_codes = {(o, h): keep.tile([P, HALF], U32, name=f"x_codes{o}{h}", align_bytes=64) for o in range(PASSES) for h in range(HALVES)}
+
+        def list_half(lst, h):
+            return lst[:, h * HALF // 16 : (h + 1) * HALF // 16]
+
+        def gather_x(o, h):
+            nc.vector.tensor_copy(x_codes[o, h][:], x_table[o][:].bitcast(U32).indirect(list_half(offs_sb, h)))
+
+        def product(a, t, h):
+            bank = psum.tile([P, HALF], F32, name="bank")
+            for o in range(PASSES):
+                nc.tensor.matmul_mx(
+                    out=bank[:],
+                    lhsT=w_codes[a, o][:, P * t : P * (t + 1)].bitcast(FP8X4),
+                    lhsT_scale=w_scales[a, o][:, P * t : P * (t + 1)],
+                    rhs=x_codes[o, h][:].bitcast(FP8X4),
+                    rhs_scale=x_scale[4 * o :, HALF * h : HALF * (h + 1)],
+                    start=(o == 0),
+                    stop=(o == PASSES - 1),
+                )
+            return bank
+
+        round_w(nc.scalar.copy, (2, 0), 0, 4)
+        nc.vector.tensor_copy(x_scale[:], scale_table[:].indirect(offs_sb[:]))
+        for h in range(HALVES):
+            gather_x(0, h)
+        quantize_w((2, 0), 0, 4)
+        round_w(nc.vector.tensor_copy, (2, 1), 0, 2)
+        round_w(nc.scalar.copy, (2, 1), 2, 4)
+        quantize_w((2, 1), 0, 2)
+        quantize_w((2, 1), 2, 4)
+
+        wet = keep.tile([P, PACK, S], F32, name="wet")
+        for h in range(HALVES):
+            gather_x(1, h)
+            for t in range(PACK):
+                bank = product(2, t, h)
+                nc.scalar.activation(wet[:, t, HALF * h : HALF * (h + 1)], bank[:], ACT.Sigmoid, scale=-1.0)
+
+        for o in range(PASSES):
+            round_w(nc.vector.tensor_copy, (1, o), 0, 4)
+        for o in range(PASSES):
+            quantize_w((1, o), 0, 4)
+        w3_bf = keep.tile([P, N, PACK], BF16, name="w3_bf", align_bytes=64)
+        w3_codes = keep.tile([P, N], U32, name="w3_codes", align_bytes=64)
+        w3_scales = keep.tile([P, N], U8, name="w3_scales", align_bytes=64)
+        nc.vector.tensor_copy(out=w3_bf[:], in_=w3_raw[:].rearrange("p j n -> p n j"))
+        nc.vector.quantize_mx(out=w3_codes[:].bitcast(FP8X4), scales=w3_scales[:], in_=w3_bf[:].rearrange("p n j -> p (n j)"))
+
+        identity = keep.tile([P, P], F32, name="identity")
+        make_identity(nc, identity[:])
+
+        wet_all = wet[:].rearrange("p t s -> p (t s)")
+        for c0, c1 in ((0, HALF), (HALF, DIRECT)):
+            nc.vector.tensor_tensor(wet_all[:, c0:c1], wet_all[:, c0:c1], wet_all[:, c0:c1], ALU.mult)
+            nc.vector.tensor_scalar(wet_all[:, c0:c1], wet_all[:, c0:c1], 1.0, None, ALU.add)
+            nc.vector.reciprocal(wet_all[:, c0:c1], wet_all[:, c0:c1])
+        nc.scalar.activation(wet_all[:, DIRECT:], wet_all[:, DIRECT:], ACT.Ln, bias=TINY)
+
+        thetae = [keep.tile([P, S], F32, name=f"thetae{t}") for t in range(PACK)]
+        temp = [keep.tile([P, S], F32, name=f"temp{t}") for t in range(PACK)]
+        stats = [keep.tile([P, 4 * V], F32, name=f"stats{t}") for t in range(PACK)]
+        planes = keep.tile([P, PACK, U], BF16, name="planes")
+        te = [keep.tile([P, S], F32, name=f"te{t}") for t in range(PACK)]
+        cape_t = {}
+
+        def activations(t):
+            banks = [product(1, t, h) for h in range(HALVES)]
+            if t == 0:
+                nc.scalar.activation(temp[t][:, :HALF], banks[0][:], ACT.Tanh)
+                nc.scalar.activation(wet[:, t, :HALF], wet[:, t, :HALF], ACT.Exp, scale=1.2, bias=-0.6)
+                nc.scalar.activation(wet[:, t, DIRECT:], wet[:, t, DIRECT:], ACT.Tanh, scale=-1.0)
+                nc.scalar.activation(temp[t][:, HALF:], banks[1][:], ACT.Tanh)
+                nc.scalar.activation(wet[:, t, DIRECT:], wet[:, t, DIRECT:], ACT.Exp, scale=0.6)
+                nc.scalar.activation(wet[:, t, HALF:DIRECT], wet[:, t, HALF:DIRECT], ACT.Exp, scale=1.2, bias=-0.6)
+            else:
+                nc.scalar.activation(wet[:, t, :], wet[:, t, :], ACT.Tanh, scale=-1.0)
+                for h in range(HALVES):
+                    nc.scalar.activation(temp[t][:, HALF * h : HALF * (h + 1)], banks[h][:], ACT.Tanh)
+                nc.scalar.activation(wet[:, t, :], wet[:, t, :], ACT.Exp, scale=0.6)
+
+        def make_thetae(t, pieces):
+            w = S // pieces
+            for h in range(pieces):
+                cols = slice(w * h, w * (h + 1))
+                nc.vector.scalar_tensor_tensor(thetae[t][:, cols], temp[t][:, cols], 1.5, wet[:, t, cols], ALU.add, ALU.mult)
+
+        def look_up_env(t, h, on_scalar):
+            picked = thetae[t][:].indirect(list_half(env_sb, h))
+            if on_scalar:
+                nc.scalar.activation(te[t][:, HALF * h : HALF * (h + 1)], picked, ACT.Copy)
+            else:
+                nc.vector.tensor_copy(te[t][:, HALF * h : HALF * (h + 1)], picked)
+
+        def reduce_levels(t, pieces):
+            sink = temp[(t + 1) % PACK]
+            lift = ring.tile([P, S], F32, name="lift")
+            cape_t[t] = psum.tile([P, HALVES, P], F32, name="bank")
+            w = S // pieces
+            g = V // pieces
+            for h in range(pieces):
+                cols = slice(w * h, w * (h + 1))
+                nc.vector.tensor_tensor(sink[:, cols], te[t][:, cols], thetae[t][:, cols], ALU.subtract)
+                nc.vector.scalar_tensor_tensor(lift[:, cols], sink[:, cols], 0.0, dz_sb[t][:, cols], ALU.min, ALU.mult)
+                sink4 = sink[:, cols].rearrange("p (v d) -> p v d", d=D)
+                worst = stats[t][:, 2 * V + 2 * g * h : 2 * V + 2 * g * (h + 1)].rearrange("p (v e) -> p v e", e=2)
+                nc.vector.tensor_tensor(worst, sink4[:, :, 0:2], sink4[:, :, 2:4], ALU.max)
+                nc.vector.scalar_tensor_tensor(stats[t][:, V + g * h : V + g * (h + 1)], worst[:, :, 0], 0.0, worst[:, :, 1], ALU.max, ALU.max)
+            nc.vector.tensor_scalar(stats[t][:, V : 2 * V], stats[t][:, V : 2 * V], unit_sb[:, t : t + 1], None, ALU.mult)
+            for h in range(HALVES):
+                for d in range(D):
+                    nc.tensor.matmul(
+                        cape_t[t][:, h, :],
+                        lift[:, HALF * h + d : HALF * (h + 1) : D],
+                        identity[:],
+                        start=(d == 0),
+                        stop=(d == D - 1),
+                        is_transpose=True,
+                    )
+
+        def make_hid(t):
+            root_t = ring.tile([P, V], F32, name="root_t")
+            nc.scalar.activation(root_t[:], cape_t[t][:].rearrange("p h i -> p (h i)"), ACT.Sqrt, scale=-1.0, bias=0.1)
+            root = psum.tile([P, V], F32, name="bank")
+            for h in range(HALVES):
+                nc.tensor.transpose(root[:, P * h : P * (h + 1)], root_t[:, P * h : P * (h + 1)], identity[:])
+            nc.vector.scalar_tensor_tensor(stats[t][:, 0:V], root[:], unit_sb[:, t : t + 1], stats[t][:, V : 2 * V], ALU.mult, ALU.subtract)
+
+        def look_up_stations(t):
+            if STN[t] == "A":
+                nc.scalar.activation(planes[:, t, :], stats[t][:].indirect(stn_sb[:]), ACT.Copy)
+            elif STN[t] == "V":
+                nc.vector.tensor_copy(planes[:, t, :], stats[t][:].indirect(stn_sb[:]))
+            else:
+                nc.vector.tensor_copy(planes[:, t, : U // 2], stats[t][:].indirect(stn_sb[:, : U // 32]))
+                nc.scalar.activation(planes[:, t, U // 2 :], stats[t][:].indirect(stn_sb[:, U // 32 :]), ACT.Copy)
+
+        for t in range(PACK):
+            activations(t)
+            make_thetae(t, 2 if t == 0 else 1)
+            if t > 0:
+                for h in range(HALVES):
+                    look_up_env(t - 1, h, ENV[2 * (t - 1) + h] == "A")
+        for h in range(HALVES):
+            look_up_env(PACK - 1, h, ENV[2 * (PACK - 1) + h] == "A")
+        for t in range(PACK):
+            if t >= LAG:
+                make_hid(t - LAG)
+            reduce_levels(t, 2 if t == PACK - 1 else 1)
+        for t in range(PACK - LAG, PACK):
+            make_hid(t)
+        for t in range(PACK):
+            look_up_stations(t)
+
+        R = U // 2
+        for h, copy in enumerate((nc.vector.tensor_copy, nc.scalar.copy)):
+            hid_bf = keep.tile([P, R, PACK], BF16, name=f"hid_bf{h}", align_bytes=64)
+            hid_codes = keep.tile([P, R], U32, name=f"hid_codes{h}", align_bytes=64)
+            hid_scales = keep.tile([P, R], U8, name=f"hid_scales{h}", align_bytes=64)
+            result = keep.tile([P, R], F32, name=f"result{h}")
+            copy(
+                out=hid_bf[:].rearrange("p (c i) t -> p c t i", i=4),
+                in_=planes[:, :, R * h : R * (h + 1)].rearrange("p t (c i) -> p c t i", i=4),
+            )
+            nc.vector.quantize_mx(out=hid_codes[:].bitcast(FP8X4), scales=hid_scales[:], in_=hid_bf[:].rearrange("p r t -> p (r t)"))
+            hazards = psum.tile([P, R], F32, name="bank")
+            nc.tensor.matmul_mx(
+                out=hazards[:],
+                lhsT=w3_codes[:].bitcast(FP8X4),
+                lhsT_scale=w3_scales[:],
+                rhs=hid_codes[:].bitcast(FP8X4),
+                rhs_scale=hid_scales[:],
+                start=True,
+                stop=True,
+            )
+            nc.scalar.copy(result[:], hazards[:])
+            nc.sync.dma_start(out=out[:, R * h : R * (h + 1)], in_=result[:])

@@ -24,8 +24,8 @@ HALVES = S // HALF
 TINY = 2.0 ** -60
 DIRECT = 768
 ENV = "VVVAAAAA"
+UNIT = "VAVV"
 STN = "AASS"
-LAG = 3
 
 
 def tile_picked_yweathr_upd_p_kernel(tc, x_words, x_scales, w1, w2, dz, unit, w3, offs, env, stn, out):
@@ -55,7 +55,7 @@ def tile_picked_yweathr_upd_p_kernel(tc, x_words, x_scales, w1, w2, dz, unit, w3
         nc.sync.dma_start(offs_sb[:], offs)
         load_w(2, w2, 0)
         for q in range(4):
-            nc.sync.dma_start(out=scale_table[32 * q : 32 * q + 8, :].bitcast(I32), in_=x_scales[:, 4 * q : 4 * q + 4, :].bitcast(I32))
+            nc.scalar.dma_start(out=scale_table[32 * q : 32 * q + 8, :].bitcast(I32), in_=x_scales[:, 4 * q : 4 * q + 4, :].bitcast(I32))
         load_x(0)
         load_w(2, w2, 1)
         load_x(1)
@@ -86,7 +86,7 @@ def tile_picked_yweathr_upd_p_kernel(tc, x_words, x_scales, w1, w2, dz, unit, w3
                 in_=w_bf[key][:, t0:t1].rearrange("p t m j -> p (t m j)"),
             )
 
-        x_scale = keep.tile([P, S], U8, name="x_scale", align_bytes=64)
+        x_scale = [keep.tile([P, HALF], U8, name=f"x_scale{h}", align_bytes=64) for h in range(HALVES)]
         x_codes = {(o, h): keep.tile([P, HALF], U32, name=f"x_codes{o}{h}", align_bytes=64) for o in range(PASSES) for h in range(HALVES)}
 
         def list_half(lst, h):
@@ -94,6 +94,9 @@ def tile_picked_yweathr_upd_p_kernel(tc, x_words, x_scales, w1, w2, dz, unit, w3
 
         def gather_x(o, h):
             nc.vector.tensor_copy(x_codes[o, h][:], x_table[o][:].bitcast(U32).indirect(list_half(offs_sb, h)))
+
+        def gather_scales(h):
+            nc.vector.tensor_copy(x_scale[h][:], scale_table[:].indirect(list_half(offs_sb, h)))
 
         def product(a, t, h):
             bank = psum.tile([P, HALF], F32, name="bank")
@@ -103,25 +106,27 @@ def tile_picked_yweathr_upd_p_kernel(tc, x_words, x_scales, w1, w2, dz, unit, w3
                     lhsT=w_codes[a, o][:, P * t : P * (t + 1)].bitcast(FP8X4),
                     lhsT_scale=w_scales[a, o][:, P * t : P * (t + 1)],
                     rhs=x_codes[o, h][:].bitcast(FP8X4),
-                    rhs_scale=x_scale[4 * o :, HALF * h : HALF * (h + 1)],
+                    rhs_scale=x_scale[h][4 * o :, :],
                     start=(o == 0),
                     stop=(o == PASSES - 1),
                 )
             return bank
 
         round_w(nc.scalar.copy, (2, 0), 0, 4)
-        nc.vector.tensor_copy(x_scale[:], scale_table[:].indirect(offs_sb[:]))
-        for h in range(HALVES):
-            gather_x(0, h)
+        gather_scales(0)
+        gather_x(0, 0)
         quantize_w((2, 0), 0, 4)
-        round_w(nc.vector.tensor_copy, (2, 1), 0, 2)
+        round_w(nc.scalar.copy, (2, 1), 0, 2)
         round_w(nc.scalar.copy, (2, 1), 2, 4)
         quantize_w((2, 1), 0, 2)
         quantize_w((2, 1), 2, 4)
 
         wet = keep.tile([P, PACK, S], F32, name="wet")
+        gather_x(1, 0)
+        gather_scales(1)
+        gather_x(0, 1)
+        gather_x(1, 1)
         for h in range(HALVES):
-            gather_x(1, h)
             for t in range(PACK):
                 bank = product(2, t, h)
                 nc.scalar.activation(wet[:, t, HALF * h : HALF * (h + 1)], bank[:], ACT.Sigmoid, scale=-1.0)
@@ -148,10 +153,12 @@ def tile_picked_yweathr_upd_p_kernel(tc, x_words, x_scales, w1, w2, dz, unit, w3
 
         thetae = [keep.tile([P, S], F32, name=f"thetae{t}") for t in range(PACK)]
         temp = [keep.tile([P, S], F32, name=f"temp{t}") for t in range(PACK)]
-        stats = [keep.tile([P, 4 * V], F32, name=f"stats{t}") for t in range(PACK)]
+        cin = [keep.tile([P, V], F32, name=f"cin{t}") for t in range(PACK)]
         planes = keep.tile([P, PACK, U], BF16, name="planes")
         te = [keep.tile([P, S], F32, name=f"te{t}") for t in range(PACK)]
         cape_t = {}
+        station_table = [te[2], te[3], te[1], te[0]]
+        root_t = [thetae[2], thetae[1], thetae[0], dz_sb[0]]
 
         def activations(t):
             banks = [product(1, t, h) for h in range(HALVES)]
@@ -181,22 +188,16 @@ def tile_picked_yweathr_upd_p_kernel(tc, x_words, x_scales, w1, w2, dz, unit, w3
             else:
                 nc.vector.tensor_copy(te[t][:, HALF * h : HALF * (h + 1)], picked)
 
-        def reduce_levels(t, pieces):
+        def sum_lift(t, pieces):
             sink = temp[(t + 1) % PACK]
             lift = ring.tile([P, S], F32, name="lift")
             cape_t[t] = psum.tile([P, HALVES, P], F32, name="bank")
             w = S // pieces
-            g = V // pieces
-            for h in range(pieces):
+            for h in reversed(range(pieces)):
                 cols = slice(w * h, w * (h + 1))
                 nc.vector.tensor_tensor(sink[:, cols], te[t][:, cols], thetae[t][:, cols], ALU.subtract)
                 nc.vector.scalar_tensor_tensor(lift[:, cols], sink[:, cols], 0.0, dz_sb[t][:, cols], ALU.min, ALU.mult)
-                sink4 = sink[:, cols].rearrange("p (v d) -> p v d", d=D)
-                worst = stats[t][:, 2 * V + 2 * g * h : 2 * V + 2 * g * (h + 1)].rearrange("p (v e) -> p v e", e=2)
-                nc.vector.tensor_tensor(worst, sink4[:, :, 0:2], sink4[:, :, 2:4], ALU.max)
-                nc.vector.scalar_tensor_tensor(stats[t][:, V + g * h : V + g * (h + 1)], worst[:, :, 0], 0.0, worst[:, :, 1], ALU.max, ALU.max)
-            nc.vector.tensor_scalar(stats[t][:, V : 2 * V], stats[t][:, V : 2 * V], unit_sb[:, t : t + 1], None, ALU.mult)
-            for h in range(HALVES):
+            for h in reversed(range(HALVES)):
                 for d in range(D):
                     nc.tensor.matmul(
                         cape_t[t][:, h, :],
@@ -207,22 +208,31 @@ def tile_picked_yweathr_upd_p_kernel(tc, x_words, x_scales, w1, w2, dz, unit, w3
                         is_transpose=True,
                     )
 
+        def worst_sink(t):
+            sink4 = temp[(t + 1) % PACK][:].rearrange("p (v d) -> p v d", d=D)
+            pairs = ring.tile([P, V, 2], F32, name="pairs")
+            nc.vector.tensor_tensor(pairs[:], sink4[:, :, 0:2], sink4[:, :, 2:4], ALU.max)
+            nc.vector.scalar_tensor_tensor(cin[t][:], pairs[:, :, 0], 0.0, pairs[:, :, 1], ALU.max, ALU.max)
+            if UNIT[t] == "V":
+                nc.vector.tensor_scalar(cin[t][:], cin[t][:], unit_sb[:, t : t + 1], None, ALU.mult)
+            else:
+                nc.scalar.activation(cin[t][:], cin[t][:], ACT.Copy, scale=unit_sb[:, t : t + 1])
+
         def make_hid(t):
-            root_t = ring.tile([P, V], F32, name="root_t")
-            nc.scalar.activation(root_t[:], cape_t[t][:].rearrange("p h i -> p (h i)"), ACT.Sqrt, scale=-1.0, bias=0.1)
+            nc.scalar.activation(root_t[t][:, :V], cape_t[t][:].rearrange("p h i -> p (h i)"), ACT.Sqrt, scale=-1.0, bias=0.1)
             root = psum.tile([P, V], F32, name="bank")
             for h in range(HALVES):
-                nc.tensor.transpose(root[:, P * h : P * (h + 1)], root_t[:, P * h : P * (h + 1)], identity[:])
-            nc.vector.scalar_tensor_tensor(stats[t][:, 0:V], root[:], unit_sb[:, t : t + 1], stats[t][:, V : 2 * V], ALU.mult, ALU.subtract)
+                nc.tensor.transpose(root[:, P * h : P * (h + 1)], root_t[t][:, P * h : P * (h + 1)], identity[:])
+            nc.vector.scalar_tensor_tensor(station_table[t][:, :V], root[:], unit_sb[:, t : t + 1], cin[t][:], ALU.mult, ALU.subtract)
 
         def look_up_stations(t):
             if STN[t] == "A":
-                nc.scalar.activation(planes[:, t, :], stats[t][:].indirect(stn_sb[:]), ACT.Copy)
+                nc.scalar.activation(planes[:, t, :], station_table[t][:].indirect(stn_sb[:]), ACT.Copy)
             elif STN[t] == "V":
-                nc.vector.tensor_copy(planes[:, t, :], stats[t][:].indirect(stn_sb[:]))
+                nc.vector.tensor_copy(planes[:, t, :], station_table[t][:].indirect(stn_sb[:]))
             else:
-                nc.vector.tensor_copy(planes[:, t, : U // 2], stats[t][:].indirect(stn_sb[:, : U // 32]))
-                nc.scalar.activation(planes[:, t, U // 2 :], stats[t][:].indirect(stn_sb[:, U // 32 :]), ACT.Copy)
+                nc.vector.tensor_copy(planes[:, t, : U // 2], station_table[t][:].indirect(stn_sb[:, : U // 32]))
+                nc.scalar.activation(planes[:, t, U // 2 :], station_table[t][:].indirect(stn_sb[:, U // 32 :]), ACT.Copy)
 
         for t in range(PACK):
             activations(t)
@@ -230,13 +240,15 @@ def tile_picked_yweathr_upd_p_kernel(tc, x_words, x_scales, w1, w2, dz, unit, w3
             if t > 0:
                 for h in range(HALVES):
                     look_up_env(t - 1, h, ENV[2 * (t - 1) + h] == "A")
-        for h in range(HALVES):
+        for h in reversed(range(HALVES)):
             look_up_env(PACK - 1, h, ENV[2 * (PACK - 1) + h] == "A")
         for t in range(PACK):
-            if t >= LAG:
-                make_hid(t - LAG)
-            reduce_levels(t, 2 if t == PACK - 1 else 1)
-        for t in range(PACK - LAG, PACK):
+            sum_lift(t, 2 if t == PACK - 1 else 1)
+            if t < 2:
+                worst_sink(t)
+        for t in range(PACK):
+            if t >= 2:
+                worst_sink(t)
             make_hid(t)
         for t in range(PACK):
             look_up_stations(t)

@@ -55,7 +55,7 @@ def tile_picked_yweathr_upd_p_kernel(tc, x_words, x_scales, w1, w2, dz, unit, w3
         nc.sync.dma_start(offs_sb[:], offs)
         load_w(2, w2, 0)
         for q in range(4):
-            nc.scalar.dma_start(out=scale_table[32 * q : 32 * q + 8, :].bitcast(I32), in_=x_scales[:, 4 * q : 4 * q + 4, :].bitcast(I32))
+            nc.sync.dma_start(out=scale_table[32 * q : 32 * q + 8, :].bitcast(I32), in_=x_scales[:, 4 * q : 4 * q + 4, :].bitcast(I32))
         load_x(0)
         load_w(2, w2, 1)
         load_x(1)

@@ -22,9 +22,11 @@ PASSES = K // (P * PACK)
 HALF = 512
 HALVES = S // HALF
 TINY = 2.0 ** -60
-DIRECT = 768
+DIRECT = 512
 ENV = "VVVAAAAA"
 UNIT = "VAVV"
+CAST = "VVAA"
+QP = ((0, 2), (2, 4))
 STN = "AASS"
 
 
@@ -39,10 +41,11 @@ def tile_picked_yweathr_upd_p_kernel(tc, x_words, x_scales, w1, w2, dz, unit, w3
         env_sb = keep.tile([P, S // 16], U16, name="env_sb")
         stn_sb = keep.tile([P, U // 16], U16, name="stn_sb")
         x_table = [keep.tile([P, T], I32, name=f"x_table{o}") for o in range(PASSES)]
+        scale_rows = keep.tile([P, T], U8, name="scale_rows")
         scale_table = keep.tile([P, T], U8, name="scale_table")
         w_raw = {(a, o): keep.tile([P, PACK, H], F32, name=f"w_raw{a}{o}") for a in (1, 2) for o in range(PASSES)}
         dz_sb = [keep.tile([P, S], F32, name=f"dz{t}") for t in range(PACK)]
-        unit_sb = keep.tile([P, PACK], F32, name="unit_sb")
+        unit_sb = [keep.tile([P, 1], F32, name=f"unit{t}") for t in range(PACK)]
         w3_raw = keep.tile([P, PACK, N], F32, name="w3_raw")
 
         def load_w(a, w, o):
@@ -53,31 +56,36 @@ def tile_picked_yweathr_upd_p_kernel(tc, x_words, x_scales, w1, w2, dz, unit, w3
 
         nc.vector.memset(scale_table[:].bitcast(I32), 0)
         nc.sync.dma_start(offs_sb[:], offs)
-        load_w(2, w2, 0)
         for q in range(4):
-            nc.sync.dma_start(out=scale_table[32 * q : 32 * q + 8, :].bitcast(I32), in_=x_scales[:, 4 * q : 4 * q + 4, :].bitcast(I32))
+            nc.sync.dma_start(out=scale_rows[32 * q : 32 * q + 8, :].bitcast(I32), in_=x_scales[:, 4 * q : 4 * q + 4, :].bitcast(I32))
+        load_w(2, w2, 0)
         load_x(0)
         load_w(2, w2, 1)
         load_x(1)
         load_w(1, w1, 0)
         load_w(1, w1, 1)
         nc.sync.dma_start(env_sb[:], env)
-        dz_rows = dz.rearrange("(p t) s -> p t s", t=PACK)
+        dz_rows = dz.rearrange("(g t e) s -> t g e s", t=PACK, e=8)
         for t in range(PACK):
-            nc.sync.dma_start(out=dz_sb[t][:], in_=dz_rows[:, t, :])
+            nc.sync.dma_start(out=dz_sb[t][:], in_=dz_rows[t])
         nc.sync.dma_start(stn_sb[:], stn)
-        nc.sync.dma_start(out=unit_sb[:], in_=unit.rearrange("(p t) o -> p (t o)", t=PACK))
-        nc.sync.dma_start(out=w3_raw[:], in_=w3.rearrange("(p j) n -> p j n", j=PACK))
+        w3_rows = w3.rearrange("(g t e) n -> t g e n", t=PACK, e=8)
+        for t in range(PACK):
+            nc.sync.dma_start(out=w3_raw[:, t, :], in_=w3_rows[t])
+        unit_rows = unit.rearrange("(g t e) o -> t g e o", t=PACK, e=8)
+        for t in range(PACK):
+            nc.sync.dma_start(out=unit_sb[t][:], in_=unit_rows[t])
 
         w_bf = {key: keep.tile([P, PACK, P, PACK], BF16, name=f"w_bf{key[0]}{key[1]}", align_bytes=64) for key in w_raw}
         w_codes = {key: keep.tile([P, H], U32, name=f"w_codes{key[0]}{key[1]}", align_bytes=64) for key in w_raw}
         w_scales = {key: keep.tile([P, H], U8, name=f"w_scales{key[0]}{key[1]}", align_bytes=64) for key in w_raw}
 
         def round_w(copy, key, t0, t1):
-            copy(
-                out=w_bf[key][:, t0:t1].rearrange("p t m j -> p m t j"),
-                in_=w_raw[key][:].rearrange("p j (m t) -> p m t j", t=PACK)[:, :, t0:t1, :],
-            )
+            for t in range(t0, t1):
+                copy(
+                    out=w_bf[key][:, t].rearrange("p (g a b) j -> p g a j b", a=2, b=4),
+                    in_=w_raw[key][:].rearrange("p j (g t a b) -> p t g a j b", t=PACK, a=2, b=4)[:, t],
+                )
 
         def quantize_w(key, t0, t1):
             nc.vector.quantize_mx(
@@ -113,13 +121,16 @@ def tile_picked_yweathr_upd_p_kernel(tc, x_words, x_scales, w1, w2, dz, unit, w3
             return bank
 
         round_w(nc.scalar.copy, (2, 0), 0, 4)
+        for q in range(4):
+            live = slice(32 * q, 32 * q + 8)
+            nc.vector.tensor_copy(scale_table[live, :].bitcast(I32), scale_rows[live, :].bitcast(I32))
         gather_scales(0)
         gather_x(0, 0)
         quantize_w((2, 0), 0, 4)
-        round_w(nc.scalar.copy, (2, 1), 0, 2)
-        round_w(nc.scalar.copy, (2, 1), 2, 4)
-        quantize_w((2, 1), 0, 2)
-        quantize_w((2, 1), 2, 4)
+        for t in range(PACK):
+            round_w(nc.vector.tensor_copy if CAST[t] == "V" else nc.scalar.copy, (2, 1), t, t + 1)
+        for t0, t1 in QP:
+            quantize_w((2, 1), t0, t1)
 
         wet = keep.tile([P, PACK, S], F32, name="wet")
         gather_x(1, 0)
@@ -138,14 +149,14 @@ def tile_picked_yweathr_upd_p_kernel(tc, x_words, x_scales, w1, w2, dz, unit, w3
         w3_bf = keep.tile([P, N, PACK], BF16, name="w3_bf", align_bytes=64)
         w3_codes = keep.tile([P, N], U32, name="w3_codes", align_bytes=64)
         w3_scales = keep.tile([P, N], U8, name="w3_scales", align_bytes=64)
-        nc.vector.tensor_copy(out=w3_bf[:], in_=w3_raw[:].rearrange("p j n -> p n j"))
+        nc.vector.tensor_copy(out=w3_bf[:].rearrange("p (c i) j -> p c j i", i=4), in_=w3_raw[:].rearrange("p j (c i) -> p c j i", i=4))
         nc.vector.quantize_mx(out=w3_codes[:].bitcast(FP8X4), scales=w3_scales[:], in_=w3_bf[:].rearrange("p n j -> p (n j)"))
 
         identity = keep.tile([P, P], F32, name="identity")
         make_identity(nc, identity[:])
 
         wet_all = wet[:].rearrange("p t s -> p (t s)")
-        for c0, c1 in ((0, HALF), (HALF, DIRECT)):
+        for c0, c1 in ((0, DIRECT),):
             nc.vector.tensor_tensor(wet_all[:, c0:c1], wet_all[:, c0:c1], wet_all[:, c0:c1], ALU.mult)
             nc.vector.tensor_scalar(wet_all[:, c0:c1], wet_all[:, c0:c1], 1.0, None, ALU.add)
             nc.vector.reciprocal(wet_all[:, c0:c1], wet_all[:, c0:c1])
@@ -168,7 +179,6 @@ def tile_picked_yweathr_upd_p_kernel(tc, x_words, x_scales, w1, w2, dz, unit, w3
                 nc.scalar.activation(wet[:, t, DIRECT:], wet[:, t, DIRECT:], ACT.Tanh, scale=-1.0)
                 nc.scalar.activation(temp[t][:, HALF:], banks[1][:], ACT.Tanh)
                 nc.scalar.activation(wet[:, t, DIRECT:], wet[:, t, DIRECT:], ACT.Exp, scale=0.6)
-                nc.scalar.activation(wet[:, t, HALF:DIRECT], wet[:, t, HALF:DIRECT], ACT.Exp, scale=1.2, bias=-0.6)
             else:
                 nc.scalar.activation(wet[:, t, :], wet[:, t, :], ACT.Tanh, scale=-1.0)
                 for h in range(HALVES):
@@ -214,16 +224,16 @@ def tile_picked_yweathr_upd_p_kernel(tc, x_words, x_scales, w1, w2, dz, unit, w3
             nc.vector.tensor_tensor(pairs[:], sink4[:, :, 0:2], sink4[:, :, 2:4], ALU.max)
             nc.vector.scalar_tensor_tensor(cin[t][:], pairs[:, :, 0], 0.0, pairs[:, :, 1], ALU.max, ALU.max)
             if UNIT[t] == "V":
-                nc.vector.tensor_scalar(cin[t][:], cin[t][:], unit_sb[:, t : t + 1], None, ALU.mult)
+                nc.vector.tensor_scalar(cin[t][:], cin[t][:], unit_sb[t][:], None, ALU.mult)
             else:
-                nc.scalar.activation(cin[t][:], cin[t][:], ACT.Copy, scale=unit_sb[:, t : t + 1])
+                nc.scalar.activation(cin[t][:], cin[t][:], ACT.Copy, scale=unit_sb[t][:])
 
         def make_hid(t):
             nc.scalar.activation(root_t[t][:, :V], cape_t[t][:].rearrange("p h i -> p (h i)"), ACT.Sqrt, scale=-1.0, bias=0.1)
             root = psum.tile([P, V], F32, name="bank")
             for h in range(HALVES):
                 nc.tensor.transpose(root[:, P * h : P * (h + 1)], root_t[t][:, P * h : P * (h + 1)], identity[:])
-            nc.vector.scalar_tensor_tensor(station_table[t][:, :V], root[:], unit_sb[:, t : t + 1], cin[t][:], ALU.mult, ALU.subtract)
+            nc.vector.scalar_tensor_tensor(station_table[t][:, :V], root[:], unit_sb[t][:], cin[t][:], ALU.mult, ALU.subtract)
 
         def look_up_stations(t):
             if STN[t] == "A":

from contextlib import ExitStack

import concourse.mybir as mybir
from concourse.masks import make_identity

K, T, S, D, N, H, V, U = 1024, 2048, 1024, 4, 128, 512, 256, 512
FLOPS = 2 * (2 * K * H * S + H * N * U)

F32 = mybir.dt.float32
BF16 = mybir.dt.bfloat16
I32 = mybir.dt.int32
U32 = mybir.dt.uint32
U16 = mybir.dt.uint16
U8 = mybir.dt.uint8
FP8X4 = mybir.dt.float8_e4m3fn_x4
ALU = mybir.AluOpType
ACT = mybir.ActivationFunctionType

P = 128
PACK = 4
PASSES = K // (P * PACK)
HALF = 512
HALVES = S // HALF
TINY = 2.0 ** -60
DIRECT = 512
ENV = "VVVAAAAA"
UNIT = "VAVV"
CAST = "VVAA"
QP = ((0, 2), (2, 4))
STN = "AASS"


def tile_picked_yweathr_upd_p_kernel(tc, x_words, x_scales, w1, w2, dz, unit, w3, offs, env, stn, out):
    nc = tc.nc
    with ExitStack() as ctx:
        keep = ctx.enter_context(tc.tile_pool(name="keep", bufs=1))
        ring = ctx.enter_context(tc.tile_pool(name="ring", bufs=2))
        psum = ctx.enter_context(tc.psum_pool(name="psum", bufs=8))

        offs_sb = keep.tile([P, S // 16], U16, name="offs_sb")
        env_sb = keep.tile([P, S // 16], U16, name="env_sb")
        stn_sb = keep.tile([P, U // 16], U16, name="stn_sb")
        x_table = [keep.tile([P, T], I32, name=f"x_table{o}") for o in range(PASSES)]
        scale_rows = keep.tile([P, T], U8, name="scale_rows")
        scale_table = keep.tile([P, T], U8, name="scale_table")
        w_raw = {(a, o): keep.tile([P, PACK, H], F32, name=f"w_raw{a}{o}") for a in (1, 2) for o in range(PASSES)}
        dz_sb = [keep.tile([P, S], F32, name=f"dz{t}") for t in range(PACK)]
        unit_sb = [keep.tile([P, 1], F32, name=f"unit{t}") for t in range(PACK)]
        w3_raw = keep.tile([P, PACK, N], F32, name="w3_raw")

        def load_w(a, w, o):
            nc.sync.dma_start(out=w_raw[a, o][:], in_=w[512 * o : 512 * (o + 1), :].rearrange("(p j) c -> p j c", j=PACK))

        def load_x(o):
            nc.sync.dma_start(out=x_table[o][:], in_=x_words[o].rearrange("p n t -> p (n t)").bitcast(I32))

        nc.vector.memset(scale_table[:].bitcast(I32), 0)
        nc.sync.dma_start(offs_sb[:], offs)
        for q in range(4):
            nc.sync.dma_start(out=scale_rows[32 * q : 32 * q + 8, :].bitcast(I32), in_=x_scales[:, 4 * q : 4 * q + 4, :].bitcast(I32))
        load_w(2, w2, 0)
        load_x(0)
        load_w(2, w2, 1)
        load_x(1)
        load_w(1, w1, 0)
        load_w(1, w1, 1)
        nc.sync.dma_start(env_sb[:], env)
        dz_rows = dz.rearrange("(g t e) s -> t g e s", t=PACK, e=8)
        for t in range(PACK):
            nc.sync.dma_start(out=dz_sb[t][:], in_=dz_rows[t])
        nc.sync.dma_start(stn_sb[:], stn)
        w3_rows = w3.rearrange("(g t e) n -> t g e n", t=PACK, e=8)
        for t in range(PACK):
            nc.sync.dma_start(out=w3_raw[:, t, :], in_=w3_rows[t])
        unit_rows = unit.rearrange("(g t e) o -> t g e o", t=PACK, e=8)
        for t in range(PACK):
            nc.sync.dma_start(out=unit_sb[t][:], in_=unit_rows[t])

        w_bf = {key: keep.tile([P, PACK, P, PACK], BF16, name=f"w_bf{key[0]}{key[1]}", align_bytes=64) for key in w_raw}
        w_codes = {key: keep.tile([P, H], U32, name=f"w_codes{key[0]}{key[1]}", align_bytes=64) for key in w_raw}
        w_scales = {key: keep.tile([P, H], U8, name=f"w_scales{key[0]}{key[1]}", align_bytes=64) for key in w_raw}

        def round_w(copy, key, t0, t1):
            for t in range(t0, t1):
                copy(
                    out=w_bf[key][:, t].rearrange("p (g a b) j -> p g a j b", a=2, b=4),
                    in_=w_raw[key][:].rearrange("p j (g t a b) -> p t g a j b", t=PACK, a=2, b=4)[:, t],
                )

        def quantize_w(key, t0, t1):
            nc.vector.quantize_mx(
                out=w_codes[key][:, P * t0 : P * t1].bitcast(FP8X4),
                scales=w_scales[key][:, P * t0 : P * t1],
                in_=w_bf[key][:, t0:t1].rearrange("p t m j -> p (t m j)"),
            )

        x_scale = [keep.tile([P, HALF], U8, name=f"x_scale{h}", align_bytes=64) for h in range(HALVES)]
        x_codes = {(o, h): keep.tile([P, HALF], U32, name=f"x_codes{o}{h}", align_bytes=64) for o in range(PASSES) for h in range(HALVES)}

        def list_half(lst, h):
            return lst[:, h * HALF // 16 : (h + 1) * HALF // 16]

        def gather_x(o, h):
            nc.vector.tensor_copy(x_codes[o, h][:], x_table[o][:].bitcast(U32).indirect(list_half(offs_sb, h)))

        def gather_scales(h):
            nc.vector.tensor_copy(x_scale[h][:], scale_table[:].indirect(list_half(offs_sb, h)))

        def product(a, t, h):
            bank = psum.tile([P, HALF], F32, name="bank")
            for o in range(PASSES):
                nc.tensor.matmul_mx(
                    out=bank[:],
                    lhsT=w_codes[a, o][:, P * t : P * (t + 1)].bitcast(FP8X4),
                    lhsT_scale=w_scales[a, o][:, P * t : P * (t + 1)],
                    rhs=x_codes[o, h][:].bitcast(FP8X4),
                    rhs_scale=x_scale[h][4 * o :, :],
                    start=(o == 0),
                    stop=(o == PASSES - 1),
                )
            return bank

        round_w(nc.scalar.copy, (2, 0), 0, 4)
        for q in range(4):
            live = slice(32 * q, 32 * q + 8)
            nc.vector.tensor_copy(scale_table[live, :].bitcast(I32), scale_rows[live, :].bitcast(I32))
        gather_scales(0)
        gather_x(0, 0)
        quantize_w((2, 0), 0, 4)
        for t in range(PACK):
            round_w(nc.vector.tensor_copy if CAST[t] == "V" else nc.scalar.copy, (2, 1), t, t + 1)
        for t0, t1 in QP:
            quantize_w((2, 1), t0, t1)

        wet = keep.tile([P, PACK, S], F32, name="wet")
        gather_x(1, 0)
        gather_scales(1)
        gather_x(0, 1)
        gather_x(1, 1)
        for h in range(HALVES):
            for t in range(PACK):
                bank = product(2, t, h)
                nc.scalar.activation(wet[:, t, HALF * h : HALF * (h + 1)], bank[:], ACT.Sigmoid, scale=-1.0)

        for o in range(PASSES):
            round_w(nc.vector.tensor_copy, (1, o), 0, 4)
        for o in range(PASSES):
            quantize_w((1, o), 0, 4)
        w3_bf = keep.tile([P, N, PACK], BF16, name="w3_bf", align_bytes=64)
        w3_codes = keep.tile([P, N], U32, name="w3_codes", align_bytes=64)
        w3_scales = keep.tile([P, N], U8, name="w3_scales", align_bytes=64)
        nc.vector.tensor_copy(out=w3_bf[:].rearrange("p (c i) j -> p c j i", i=4), in_=w3_raw[:].rearrange("p j (c i) -> p c j i", i=4))
        nc.vector.quantize_mx(out=w3_codes[:].bitcast(FP8X4), scales=w3_scales[:], in_=w3_bf[:].rearrange("p n j -> p (n j)"))

        identity = keep.tile([P, P], F32, name="identity")
        make_identity(nc, identity[:])

        wet_all = wet[:].rearrange("p t s -> p (t s)")
        for c0, c1 in ((0, DIRECT),):
            nc.vector.tensor_tensor(wet_all[:, c0:c1], wet_all[:, c0:c1], wet_all[:, c0:c1], ALU.mult)
            nc.vector.tensor_scalar(wet_all[:, c0:c1], wet_all[:, c0:c1], 1.0, None, ALU.add)
            nc.vector.reciprocal(wet_all[:, c0:c1], wet_all[:, c0:c1])
        nc.scalar.activation(wet_all[:, DIRECT:], wet_all[:, DIRECT:], ACT.Ln, bias=TINY)

        thetae = [keep.tile([P, S], F32, name=f"thetae{t}") for t in range(PACK)]
        temp = [keep.tile([P, S], F32, name=f"temp{t}") for t in range(PACK)]
        cin = [keep.tile([P, V], F32, name=f"cin{t}") for t in range(PACK)]
        planes = keep.tile([P, PACK, U], BF16, name="planes")
        te = [keep.tile([P, S], F32, name=f"te{t}") for t in range(PACK)]
        cape_t = {}
        station_table = [te[2], te[3], te[1], te[0]]
        root_t = [thetae[2], thetae[1], thetae[0], dz_sb[0]]

        def activations(t):
            banks = [product(1, t, h) for h in range(HALVES)]
            if t == 0:
                nc.scalar.activation(temp[t][:, :HALF], banks[0][:], ACT.Tanh)
                nc.scalar.activation(wet[:, t, :HALF], wet[:, t, :HALF], ACT.Exp, scale=1.2, bias=-0.6)
                nc.scalar.activation(wet[:, t, DIRECT:], wet[:, t, DIRECT:], ACT.Tanh, scale=-1.0)
                nc.scalar.activation(temp[t][:, HALF:], banks[1][:], ACT.Tanh)
                nc.scalar.activation(wet[:, t, DIRECT:], wet[:, t, DIRECT:], ACT.Exp, scale=0.6)
            else:
                nc.scalar.activation(wet[:, t, :], wet[:, t, :], ACT.Tanh, scale=-1.0)
                for h in range(HALVES):
                    nc.scalar.activation(temp[t][:, HALF * h : HALF * (h + 1)], banks[h][:], ACT.Tanh)
                nc.scalar.activation(wet[:, t, :], wet[:, t, :], ACT.Exp, scale=0.6)

        def make_thetae(t, pieces):
            w = S // pieces
            for h in range(pieces):
                cols = slice(w * h, w * (h + 1))
                nc.vector.scalar_tensor_tensor(thetae[t][:, cols], temp[t][:, cols], 1.5, wet[:, t, cols], ALU.add, ALU.mult)

        def look_up_env(t, h, on_scalar):
            picked = thetae[t][:].indirect(list_half(env_sb, h))
            if on_scalar:
                nc.scalar.activation(te[t][:, HALF * h : HALF * (h + 1)], picked, ACT.Copy)
            else:
                nc.vector.tensor_copy(te[t][:, HALF * h : HALF * (h + 1)], picked)

        def sum_lift(t, pieces):
            sink = temp[(t + 1) % PACK]
            lift = ring.tile([P, S], F32, name="lift")
            cape_t[t] = psum.tile([P, HALVES, P], F32, name="bank")
            w = S // pieces
            for h in reversed(range(pieces)):
                cols = slice(w * h, w * (h + 1))
                nc.vector.tensor_tensor(sink[:, cols], te[t][:, cols], thetae[t][:, cols], ALU.subtract)
                nc.vector.scalar_tensor_tensor(lift[:, cols], sink[:, cols], 0.0, dz_sb[t][:, cols], ALU.min, ALU.mult)
            for h in reversed(range(HALVES)):
                for d in range(D):
                    nc.tensor.matmul(
                        cape_t[t][:, h, :],
                        lift[:, HALF * h + d : HALF * (h + 1) : D],
                        identity[:],
                        start=(d == 0),
                        stop=(d == D - 1),
                        is_transpose=True,
                    )

        def worst_sink(t):
            sink4 = temp[(t + 1) % PACK][:].rearrange("p (v d) -> p v d", d=D)
            pairs = ring.tile([P, V, 2], F32, name="pairs")
            nc.vector.tensor_tensor(pairs[:], sink4[:, :, 0:2], sink4[:, :, 2:4], ALU.max)
            nc.vector.scalar_tensor_tensor(cin[t][:], pairs[:, :, 0], 0.0, pairs[:, :, 1], ALU.max, ALU.max)
            if UNIT[t] == "V":
                nc.vector.tensor_scalar(cin[t][:], cin[t][:], unit_sb[t][:], None, ALU.mult)
            else:
                nc.scalar.activation(cin[t][:], cin[t][:], ACT.Copy, scale=unit_sb[t][:])

        def make_hid(t):
            nc.scalar.activation(root_t[t][:, :V], cape_t[t][:].rearrange("p h i -> p (h i)"), ACT.Sqrt, scale=-1.0, bias=0.1)
            root = psum.tile([P, V], F32, name="bank")
            for h in range(HALVES):
                nc.tensor.transpose(root[:, P * h : P * (h + 1)], root_t[t][:, P * h : P * (h + 1)], identity[:])
            nc.vector.scalar_tensor_tensor(station_table[t][:, :V], root[:], unit_sb[t][:], cin[t][:], ALU.mult, ALU.subtract)

        def look_up_stations(t):
            if STN[t] == "A":
                nc.scalar.activation(planes[:, t, :], station_table[t][:].indirect(stn_sb[:]), ACT.Copy)
            elif STN[t] == "V":
                nc.vector.tensor_copy(planes[:, t, :], station_table[t][:].indirect(stn_sb[:]))
            else:
                nc.vector.tensor_copy(planes[:, t, : U // 2], station_table[t][:].indirect(stn_sb[:, : U // 32]))
                nc.scalar.activation(planes[:, t, U // 2 :], station_table[t][:].indirect(stn_sb[:, U // 32 :]), ACT.Copy)

        for t in range(PACK):
            activations(t)
            make_thetae(t, 2 if t == 0 else 1)
            if t > 0:
                for h in range(HALVES):
                    look_up_env(t - 1, h, ENV[2 * (t - 1) + h] == "A")
        for h in reversed(range(HALVES)):
            look_up_env(PACK - 1, h, ENV[2 * (PACK - 1) + h] == "A")
        for t in range(PACK):
            sum_lift(t, 2 if t == PACK - 1 else 1)
            if t < 2:
                worst_sink(t)
        for t in range(PACK):
            if t >= 2:
                worst_sink(t)
            make_hid(t)
        for t in range(PACK):
            look_up_stations(t)

        R = U // 2
        for h, copy in enumerate((nc.vector.tensor_copy, nc.scalar.copy)):
            hid_bf = keep.tile([P, R, PACK], BF16, name=f"hid_bf{h}", align_bytes=64)
            hid_codes = keep.tile([P, R], U32, name=f"hid_codes{h}", align_bytes=64)
            hid_scales = keep.tile([P, R], U8, name=f"hid_scales{h}", align_bytes=64)
            result = keep.tile([P, R], F32, name=f"result{h}")
            copy(
                out=hid_bf[:].rearrange("p (c i) t -> p c t i", i=4),
                in_=planes[:, :, R * h : R * (h + 1)].rearrange("p t (c i) -> p c t i", i=4),
            )
            nc.vector.quantize_mx(out=hid_codes[:].bitcast(FP8X4), scales=hid_scales[:], in_=hid_bf[:].rearrange("p r t -> p (r t)"))
            hazards = psum.tile([P, R], F32, name="bank")
            nc.tensor.matmul_mx(
                out=hazards[:],
                lhsT=w3_codes[:].bitcast(FP8X4),
                lhsT_scale=w3_scales[:],
                rhs=hid_codes[:].bitcast(FP8X4),
                rhs_scale=hid_scales[:],
                start=True,
                stop=True,
            )
            nc.scalar.copy(result[:], hazards[:])
            nc.sync.dma_start(out=out[:, R * h : R * (h + 1)], in_=result[:])
